import numpy as np
import ml_dtypes


def mxq(x, axis, fmt="e4m3"):
    dtype, down = {"e4m3": (ml_dtypes.float8_e4m3fn, 7), "e5m2": (ml_dtypes.float8_e5m2, 14)}[fmt]
    v = np.moveaxis(np.asarray(x, np.float32).astype(ml_dtypes.bfloat16).astype(np.float64), axis, -1)
    blocks = v.reshape(v.shape[:-1] + (-1, 32))
    amax = np.abs(blocks).max(-1, keepdims=True)
    byte = np.maximum(np.where(amax > 0, np.frexp(amax)[1] - 1 + 127, 0) - down, 1)
    scale = np.exp2(byte - 127.0)
    codes = (blocks / scale).astype(np.float32).astype(dtype).astype(np.float64)
    return np.moveaxis((codes * scale).reshape(v.shape), -1, axis)


WIDE = False


def mx_kscale(k):
    if not WIDE:
        return np.ones(k)
    levels = np.array([10, -10, 5, -5, 0])
    if k % 512:
        return np.exp2(np.random.permutation(np.resize(levels, k // 32))).repeat(32)
    a = np.empty((k // 512, 16))
    for p in range(k // 512):
        a[p, :8] = np.random.permutation(np.resize(levels, 8))
        for g in range(8):
            far = levels[np.abs(levels - a[p, g]) >= 10]
            a[p, g + 8] = far[np.random.randint(len(far))]
    return np.exp2(a.ravel()).repeat(32)


def f64(x):
    return np.asarray(x).astype(np.float64)


def striped(idx):
    return np.tile(idx.reshape(-1, 16).T, (8, 1)).astype(np.uint16)


def unstriped(offs):
    return offs[:16].T.reshape(-1).astype(np.int64)


def silu(v):
    return v / (1.0 + np.exp(-np.maximum(v, -700.0)))


K, T, S, H, N = 1024, 2048, 1024, 512, 256


def setup_inputs():
    n = np.random.standard_normal
    s = mx_kscale(K)[:, None]
    u = mx_kscale(H)
    return {
        "xT": (n((K, S)) * s).astype(np.float32),
        "w1": (n((K, H)) / np.sqrt(K) / s * u).astype(np.float32),
        "w2": (n((H, N)) / np.sqrt(H) / u[:, None]).astype(np.float32),
        "gate": np.tile(np.random.uniform(0.2, 1.0, S), (N, 1)).astype(np.float32),
        "offs": striped(np.random.permutation(T)[:S]),
    }


def reference(xT, w1, w2, gate, offs):
    idx = unstriped(offs)
    xq = mxq(f64(xT), 0, "e4m3")
    h = silu(mxq(f64(w1), 0, "e4m3").T @ xq)
    y = mxq(f64(w2), 0, "e4m3").T @ mxq(h, 0, "e4m3")
    out = np.zeros((N, T))
    out[:, idx] = f64(gate) * y
    return out

@@ -1,0 +1,211 @@
+from contextlib import ExitStack
+
+import concourse.mybir as mybir
+
+K, T, S, H, N = 1024, 2048, 1024, 512, 256
+
+FLOPS = 2 * S * H * (K + N)
+
+F32 = mybir.dt.float32
+BF16 = mybir.dt.bfloat16
+U32 = mybir.dt.uint32
+U16 = mybir.dt.uint16
+U8 = mybir.dt.uint8
+FP8X4 = mybir.dt.float8_e4m3fn_x4
+MULT = mybir.AluOpType.mult
+SILU = mybir.ActivationFunctionType.Silu
+
+P = 128
+CH = 256
+NCH = S // CH
+NT = 128
+
+
+def tile_picked_place_mlp_silu_sub_l_kernel(tc, xT, w1, w2, gate, offs, out):
+    nc = tc.nc
+    with ExitStack() as ctx:
+        keep = ctx.enter_context(tc.tile_pool(name="keep", bufs=1))
+        hpool = ctx.enter_context(tc.tile_pool(name="hpool", bufs=2))
+        ypool = ctx.enter_context(tc.tile_pool(name="ypool", bufs=4))
+        psum = ctx.enter_context(tc.psum_pool(name="psum", bufs=4))
+
+        offsets = keep.tile([P, S // 16], U16, name="offsets")
+        windows = [keep.tile([P, T], F32, name=f"window{m}") for m in range(2)]
+        gates = keep.tile([P, 2, S], F32, name="gates")
+        w1_raw = [keep.tile([P, 4, H], F32, name=f"w1_raw{g}") for g in range(2)]
+        w2_raw = keep.tile([P, 4, N], F32, name="w2_raw")
+        x_raw = [[keep.tile([P, 4, CH], F32, name=f"x_raw{c}_{g}") for g in range(2)] for c in range(NCH)]
+
+        def load_x(c, g):
+            src = xT[512 * g : 512 * (g + 1), CH * c : CH * (c + 1)]
+            nc.sync.dma_start(out=x_raw[c][g][:], in_=src.rearrange("(p j) s -> p j s", j=4))
+
+        def load_w1(g):
+            nc.sync.dma_start(out=w1_raw[g][:], in_=w1[512 * g : 512 * (g + 1), :].rearrange("(p j) h -> p j h", j=4))
+
+        gate_v = gate.rearrange("(m p) s -> p m s", m=2)
+        load_w1(0)
+        load_w1(1)
+        load_x(0, 0)
+        load_x(0, 1)
+        nc.sync.dma_start(out=w2_raw[:], in_=w2.rearrange("(p j) n -> p j n", j=4))
+        load_x(1, 0)
+        load_x(1, 1)
+        nc.sync.dma_start(offsets[:], offs)
+        nc.sync.dma_start(out=gates[:, :, 0:CH], in_=gate_v[:, :, 0:CH])
+        load_x(2, 0)
+        load_x(2, 1)
+        nc.sync.dma_start(out=gates[:, :, CH:S], in_=gate_v[:, :, CH:S])
+        load_x(3, 0)
+        load_x(3, 1)
+
+        warm = keep.tile([P, 2], F32, name="warm")
+        nc.vector.memset(warm[:], 0.0)
+        nc.scalar.activation(warm[:, 1:2], warm[:, 0:1], SILU)
+        for m in range(2):
+            nc.vector.memset(windows[m][:], 0.0)
+
+        w1_grp = [keep.tile([P, 4 * H], BF16, name=f"w1_grp{g}", align_bytes=64) for g in range(2)]
+        w1_codes = [keep.tile([P, H], U32, name=f"w1_codes{g}", align_bytes=64) for g in range(2)]
+        w1_scales = [keep.tile([P, H], U8, name=f"w1_scales{g}", align_bytes=64) for g in range(2)]
+        w2_grp = keep.tile([P, N, 4], BF16, name="w2_grp", align_bytes=64)
+        w2_codes = keep.tile([P, N], U32, name="w2_codes", align_bytes=64)
+        w2_scales = keep.tile([P, N], U8, name="w2_scales", align_bytes=64)
+        x_grp = [[keep.tile([P, CH, 4], BF16, name=f"x_grp{c}_{g}", align_bytes=64) for g in range(2)] for c in range(NCH)]
+        x_codes = [[keep.tile([P, CH], U32, name=f"x_codes{c}_{g}", align_bytes=64) for g in range(2)] for c in range(NCH)]
+        x_scales = [[keep.tile([P, CH], U8, name=f"x_scales{c}_{g}", align_bytes=64) for g in range(2)] for c in range(NCH)]
+
+        def copy_on(engine, dst, src):
+            if engine == "v":
+                nc.vector.tensor_copy(out=dst, in_=src)
+            else:
+                nc.scalar.copy(out=dst, in_=src)
+
+        def quantize(codes, scales, grouped):
+            nc.vector.quantize_mx(out=codes.bitcast(FP8X4), scales=scales, in_=grouped)
+
+        def copy_w1(g, engine, m0, m1):
+            dst = w1_grp[g][:].rearrange("p (t m j) -> p m j t", t=4, j=4)
+            src = w1_raw[g][:].rearrange("p j (m t) -> p m j t", t=4)
+            copy_on(engine, dst[:, m0:m1], src[:, m0:m1])
+
+        def copy_x(c, g, engine, a, b):
+            dst = x_grp[c][g][:, a:b, :].rearrange("p (n i) j -> p n j i", i=4)
+            src = x_raw[c][g][:, :, a:b].rearrange("p j (n i) -> p n j i", i=4)
+            copy_on(engine, dst, src)
+
+        def quant_x(c, g, a, b):
+            quantize(x_codes[c][g][:, a:b], x_scales[c][g][:, a:b], x_grp[c][g][:, a:b, :].rearrange("p n j -> p (n j)"))
+
+        def layer1(c):
+            banks = []
+            for b in range(CH // NT):
+                bank = psum.tile([P, 4, NT], F32, name="h_bank")
+                cols = slice(NT * b, NT * (b + 1))
+                for t in range(4):
+                    for g in range(2):
+                        nc.tensor.matmul_mx(
+                            out=bank[:, t, :],
+                            lhsT=w1_codes[g][:, P * t : P * (t + 1)].bitcast(FP8X4),
+                            lhsT_scale=w1_scales[g][:, P * t : P * (t + 1)],
+                            rhs=x_codes[c][g][:, cols].bitcast(FP8X4),
+                            rhs_scale=x_scales[c][g][:, cols],
+                            start=(g == 0),
+                            stop=(g == 1),
+                        )
+                banks.append(bank)
+            return banks
+
+        def silu(banks):
+            h_grp = hpool.tile([P, CH, 4], BF16, name="h_grp", align_bytes=64)
+            for b in range(CH // NT):
+                nc.scalar.activation(h_grp[:, NT * b : NT * (b + 1), :], banks[b][:].rearrange("p t n -> p n t"), SILU)
+            return h_grp
+
+        def quant_h(h_grp):
+            codes = hpool.tile([P, CH], U32, name="h_codes", align_bytes=64)
+            scales = hpool.tile([P, CH], U8, name="h_scales", align_bytes=64)
+            quantize(codes[:], scales[:], h_grp[:].rearrange("p n j -> p (n j)"))
+            return codes, scales
+
+        def layer2(hq):
+            codes, scales = hq
+            ys = []
+            for m in range(2):
+                y_bank = psum.tile([P, CH], F32, name="y_bank")
+                nc.tensor.matmul_mx(
+                    out=y_bank[:],
+                    lhsT=w2_codes[:, P * m : P * (m + 1)].bitcast(FP8X4),
+                    lhsT_scale=w2_scales[:, P * m : P * (m + 1)],
+                    rhs=codes[:].bitcast(FP8X4),
+                    rhs_scale=scales[:],
+                    start=True,
+                    stop=True,
+                )
+                y = ypool.tile([P, CH], F32, name="y")
+                nc.scalar.copy(out=y[:], in_=y_bank[:])
+                ys.append(y)
+            return ys
+
+        def scatter(c, m, y):
+            ents = offsets[:, CH // 16 * c : CH // 16 * (c + 1)]
+            nc.vector.tensor_tensor(windows[m][:].indirect(ents), y[:], gates[:, m, CH * c : CH * (c + 1)], MULT)
+
+        A, B = (0, 128), (128, 256)
+        copy_w1(0, "v", 0, 64)
+        copy_w1(0, "s", 64, 128)
+        quantize(w1_codes[0][:], w1_scales[0][:], w1_grp[0][:])
+        copy_w1(1, "v", 0, 64)
+        copy_w1(1, "s", 64, 128)
+        copy_x(0, 0, "s", *A)
+        copy_x(0, 0, "v", *B)
+        quantize(w1_codes[1][:], w1_scales[1][:], w1_grp[1][:])
+        quant_x(0, 0, 0, 256)
+        copy_x(0, 1, "v", *A)
+        copy_x(0, 1, "s", *B)
+        quant_x(0, 1, *A)
+        quant_x(0, 1, *B)
+        h0 = layer1(0)
+        w2_dst = w2_grp[:].rearrange("p (n i) j -> p n j i", i=4)
+        w2_src = w2_raw[:].rearrange("p j (n i) -> p n j i", i=4)
+        copy_on("v", w2_dst, w2_src)
+        copy_x(1, 0, "v", *B)
+        quantize(w2_codes[:], w2_scales[:], w2_grp[:].rearrange("p n j -> p (n j)"))
+        hq = quant_h(silu(h0))
+        copy_x(1, 0, "v", *A)
+        copy_x(1, 1, "v", *A)
+        copy_x(1, 1, "s", *B)
+        quant_x(1, 0, 0, CH)
+        quant_x(1, 1, 0, CH)
+        ys = layer2(hq)
+        hb = layer1(1)
+        scatter(0, 0, ys[0])
+        copy_x(2, 0, "s", *A)
+        copy_x(2, 0, "s", *B)
+        scatter(0, 1, ys[1])
+        hq = quant_h(silu(hb))
+        copy_x(2, 1, "s", *B)
+        copy_x(2, 1, "v", *A)
+        ys = layer2(hq)
+        quant_x(2, 0, 0, CH)
+        quant_x(2, 1, 0, CH)
+        hb = layer1(2)
+        scatter(1, 0, ys[0])
+        copy_x(3, 0, "s", *A)
+        copy_x(3, 0, "s", *B)
+        quant_x(3, 0, 0, CH)
+        scatter(1, 1, ys[1])
+        hq = quant_h(silu(hb))
+        copy_x(3, 1, "s", *A)
+        copy_x(3, 1, "s", *B)
+        ys = layer2(hq)
+        quant_x(3, 1, 0, CH)
+        hb = layer1(3)
+        scatter(2, 0, ys[0])
+        hq = quant_h(silu(hb))
+        scatter(2, 1, ys[1])
+        ys = layer2(hq)
+        scatter(3, 0, ys[0])
+        scatter(3, 1, ys[1])
+        for m in range(2):
+            nc.sync.dma_start(out=out[P * m : P * (m + 1), :], in_=windows[m][:])

@@ -25,8 +25,8 @@ def tile_picked_place_mlp_silu_sub_l_kernel(tc, xT, w1, w2, gate, offs, out):
     nc = tc.nc
     with ExitStack() as ctx:
         keep = ctx.enter_context(tc.tile_pool(name="keep", bufs=1))
-        hpool = ctx.enter_context(tc.tile_pool(name="hpool", bufs=2))
-        ypool = ctx.enter_context(tc.tile_pool(name="ypool", bufs=4))
+        hpool = ctx.enter_context(tc.tile_pool(name="hpool", bufs=4))
+        ypool = ctx.enter_context(tc.tile_pool(name="ypool", bufs=8))
         psum = ctx.enter_context(tc.psum_pool(name="psum", bufs=4))
 
         offsets = keep.tile([P, S // 16], U16, name="offsets")
@@ -55,9 +55,9 @@ def tile_picked_place_mlp_silu_sub_l_kernel(tc, xT, w1, w2, gate, offs, out):
         nc.sync.dma_start(out=gates[:, :, 0:CH], in_=gate_v[:, :, 0:CH])
         load_x(2, 0)
         load_x(2, 1)
-        nc.sync.dma_start(out=gates[:, :, CH:S], in_=gate_v[:, :, CH:S])
         load_x(3, 0)
         load_x(3, 1)
+        nc.sync.dma_start(out=gates[:, :, CH:S], in_=gate_v[:, :, CH:S])
 
         warm = keep.tile([P, 2], F32, name="warm")
         nc.vector.memset(warm[:], 0.0)
@@ -71,9 +71,9 @@ def tile_picked_place_mlp_silu_sub_l_kernel(tc, xT, w1, w2, gate, offs, out):
         w2_grp = keep.tile([P, N, 4], BF16, name="w2_grp", align_bytes=64)
         w2_codes = keep.tile([P, N], U32, name="w2_codes", align_bytes=64)
         w2_scales = keep.tile([P, N], U8, name="w2_scales", align_bytes=64)
-        x_grp = [[keep.tile([P, CH, 4], BF16, name=f"x_grp{c}_{g}", align_bytes=64) for g in range(2)] for c in range(NCH)]
-        x_codes = [[keep.tile([P, CH], U32, name=f"x_codes{c}_{g}", align_bytes=64) for g in range(2)] for c in range(NCH)]
-        x_scales = [[keep.tile([P, CH], U8, name=f"x_scales{c}_{g}", align_bytes=64) for g in range(2)] for c in range(NCH)]
+        x_grp = [keep.tile([P, 2, CH, 4], BF16, name=f"x_grp{c}", align_bytes=64) for c in range(NCH)]
+        x_codes = [keep.tile([P, 2, CH], U32, name=f"x_codes{c}", align_bytes=64) for c in range(NCH)]
+        x_scales = [keep.tile([P, 2, CH], U8, name=f"x_scales{c}", align_bytes=64) for c in range(NCH)]
 
         def copy_on(engine, dst, src):
             if engine == "v":
@@ -90,12 +90,19 @@ def tile_picked_place_mlp_silu_sub_l_kernel(tc, xT, w1, w2, gate, offs, out):
             copy_on(engine, dst[:, m0:m1], src[:, m0:m1])
 
         def copy_x(c, g, engine, a, b):
-            dst = x_grp[c][g][:, a:b, :].rearrange("p (n i) j -> p n j i", i=4)
+            dst = x_grp[c][:, g, a:b, :].rearrange("p (n i) j -> p n j i", i=4)
             src = x_raw[c][g][:, :, a:b].rearrange("p j (n i) -> p n j i", i=4)
             copy_on(engine, dst, src)
 
         def quant_x(c, g, a, b):
-            quantize(x_codes[c][g][:, a:b], x_scales[c][g][:, a:b], x_grp[c][g][:, a:b, :].rearrange("p n j -> p (n j)"))
+            quantize(x_codes[c][:, g, a:b], x_scales[c][:, g, a:b], x_grp[c][:, g, a:b, :].rearrange("p n j -> p (n j)"))
+
+        def quant_x_both(c):
+            quantize(
+                x_codes[c][:].rearrange("p g n -> p (g n)"),
+                x_scales[c][:].rearrange("p g n -> p (g n)"),
+                x_grp[c][:].rearrange("p g n j -> p (g n j)"),
+            )
 
         def layer1(c):
             banks = []
@@ -108,8 +115,8 @@ def tile_picked_place_mlp_silu_sub_l_kernel(tc, xT, w1, w2, gate, offs, out):
                             out=bank[:, t, :],
                             lhsT=w1_codes[g][:, P * t : P * (t + 1)].bitcast(FP8X4),
                             lhsT_scale=w1_scales[g][:, P * t : P * (t + 1)],
-                            rhs=x_codes[c][g][:, cols].bitcast(FP8X4),
-                            rhs_scale=x_scales[c][g][:, cols],
+                            rhs=x_codes[c][:, g, cols].bitcast(FP8X4),
+                            rhs_scale=x_scales[c][:, g, cols],
                             start=(g == 0),
                             stop=(g == 1),
                         )
@@ -128,84 +135,103 @@ def tile_picked_place_mlp_silu_sub_l_kernel(tc, xT, w1, w2, gate, offs, out):
             quantize(codes[:], scales[:], h_grp[:].rearrange("p n j -> p (n j)"))
             return codes, scales
 
-        def layer2(hq):
+        def layer2(hq, m):
             codes, scales = hq
-            ys = []
-            for m in range(2):
-                y_bank = psum.tile([P, CH], F32, name="y_bank")
-                nc.tensor.matmul_mx(
-                    out=y_bank[:],
-                    lhsT=w2_codes[:, P * m : P * (m + 1)].bitcast(FP8X4),
-                    lhsT_scale=w2_scales[:, P * m : P * (m + 1)],
-                    rhs=codes[:].bitcast(FP8X4),
-                    rhs_scale=scales[:],
-                    start=True,
-                    stop=True,
-                )
-                y = ypool.tile([P, CH], F32, name="y")
-                nc.scalar.copy(out=y[:], in_=y_bank[:])
-                ys.append(y)
-            return ys
+            y_bank = psum.tile([P, CH], F32, name="y_bank")
+            nc.tensor.matmul_mx(
+                out=y_bank[:],
+                lhsT=w2_codes[:, P * m : P * (m + 1)].bitcast(FP8X4),
+                lhsT_scale=w2_scales[:, P * m : P * (m + 1)],
+                rhs=codes[:].bitcast(FP8X4),
+                rhs_scale=scales[:],
+                start=True,
+                stop=True,
+            )
+            return y_bank
+
+        def fetch(y_bank):
+            y = ypool.tile([P, CH], F32, name="y")
+            nc.scalar.copy(out=y[:], in_=y_bank[:])
+            return y
+
+        def copy_w2(engine, a, b):
+            dst = w2_grp[:, a:b, :].rearrange("p (n i) j -> p n j i", i=4)
+            src = w2_raw[:, :, a:b].rearrange("p j (n i) -> p n j i", i=4)
+            copy_on(engine, dst, src)
+
+        def store(m):
+            nc.sync.dma_start(out=out[P * m : P * (m + 1), :], in_=windows[m][:])
 
         def scatter(c, m, y):
             ents = offsets[:, CH // 16 * c : CH // 16 * (c + 1)]
             nc.vector.tensor_tensor(windows[m][:].indirect(ents), y[:], gates[:, m, CH * c : CH * (c + 1)], MULT)
 
-        A, B = (0, 128), (128, 256)
+        A, B, AB = (0, 128), (128, 256), (0, 256)
         copy_w1(0, "v", 0, 64)
         copy_w1(0, "s", 64, 128)
         quantize(w1_codes[0][:], w1_scales[0][:], w1_grp[0][:])
         copy_w1(1, "v", 0, 64)
         copy_w1(1, "s", 64, 128)
-        copy_x(0, 0, "s", *A)
-        copy_x(0, 0, "v", *B)
+        copy_x(0, 0, "v", *A)
+        copy_x(0, 0, "s", *B)
         quantize(w1_codes[1][:], w1_scales[1][:], w1_grp[1][:])
-        quant_x(0, 0, 0, 256)
+        quant_x(0, 0, *AB)
         copy_x(0, 1, "v", *A)
         copy_x(0, 1, "s", *B)
         quant_x(0, 1, *A)
         quant_x(0, 1, *B)
-        h0 = layer1(0)
-        w2_dst = w2_grp[:].rearrange("p (n i) j -> p n j i", i=4)
-        w2_src = w2_raw[:].rearrange("p j (n i) -> p n j i", i=4)
-        copy_on("v", w2_dst, w2_src)
-        copy_x(1, 0, "v", *B)
+        banks0 = layer1(0)
+        copy_w2("v", *B)
+        copy_w2("s", *A)
         quantize(w2_codes[:], w2_scales[:], w2_grp[:].rearrange("p n j -> p (n j)"))
-        hq = quant_h(silu(h0))
-        copy_x(1, 0, "v", *A)
-        copy_x(1, 1, "v", *A)
-        copy_x(1, 1, "s", *B)
-        quant_x(1, 0, 0, CH)
-        quant_x(1, 1, 0, CH)
-        ys = layer2(hq)
-        hb = layer1(1)
-        scatter(0, 0, ys[0])
-        copy_x(2, 0, "s", *A)
+        h0 = silu(banks0)
+        copy_x(1, 0, "v", *AB)
+        copy_x(1, 1, "v", *B)
+        copy_x(1, 1, "s", *A)
+        quant_x(1, 0, *AB)
+        hq0 = quant_h(h0)
+        y_bank00 = layer2(hq0, 0)
+        y_bank01 = layer2(hq0, 1)
+        quant_x(1, 1, *AB)
+        banks1 = layer1(1)
+        y00 = fetch(y_bank00)
         copy_x(2, 0, "s", *B)
-        scatter(0, 1, ys[1])
-        hq = quant_h(silu(hb))
+        copy_x(2, 0, "v", *A)
+        scatter(0, 0, y00)
+        h1 = silu(banks1)
         copy_x(2, 1, "s", *B)
+        y01 = fetch(y_bank01)
         copy_x(2, 1, "v", *A)
-        ys = layer2(hq)
-        quant_x(2, 0, 0, CH)
-        quant_x(2, 1, 0, CH)
-        hb = layer1(2)
-        scatter(1, 0, ys[0])
-        copy_x(3, 0, "s", *A)
-        copy_x(3, 0, "s", *B)
-        quant_x(3, 0, 0, CH)
-        scatter(1, 1, ys[1])
-        hq = quant_h(silu(hb))
+        hq1 = quant_h(h1)
+        y_bank10 = layer2(hq1, 0)
+        y_bank11 = layer2(hq1, 1)
+        quant_x_both(2)
+        banks2 = layer1(2)
+        copy_x(3, 0, "s", *AB)
+        scatter(0, 1, y01)
         copy_x(3, 1, "s", *A)
-        copy_x(3, 1, "s", *B)
-        ys = layer2(hq)
-        quant_x(3, 1, 0, CH)
-        hb = layer1(3)
-        scatter(2, 0, ys[0])
-        hq = quant_h(silu(hb))
-        scatter(2, 1, ys[1])
-        ys = layer2(hq)
-        scatter(3, 0, ys[0])
-        scatter(3, 1, ys[1])
-        for m in range(2):
-            nc.sync.dma_start(out=out[P * m : P * (m + 1), :], in_=windows[m][:])
+        copy_x(3, 1, "v", *B)
+        y10 = fetch(y_bank10)
+        y11 = fetch(y_bank11)
+        quant_x_both(3)
+        banks3 = layer1(3)
+        scatter(1, 0, y10)
+        h2 = silu(banks2)
+        h3 = silu(banks3)
+        hq2 = quant_h(h2)
+        y_bank20 = layer2(hq2, 0)
+        y_bank21 = layer2(hq2, 1)
+        scatter(1, 1, y11)
+        y20 = fetch(y_bank20)
+        y21 = fetch(y_bank21)
+        hq3 = quant_h(h3)
+        y_bank30 = layer2(hq3, 0)
+        y_bank31 = layer2(hq3, 1)
+        scatter(2, 0, y20)
+        y30 = fetch(y_bank30)
+        y31 = fetch(y_bank31)
+        scatter(3, 0, y30)
+        store(0)
+        scatter(2, 1, y21)
+        scatter(3, 1, y31)
+        store(1)

from contextlib import ExitStack

import concourse.mybir as mybir

K, T, S, H, N = 1024, 2048, 1024, 512, 256

FLOPS = 2 * S * H * (K + N)

F32 = mybir.dt.float32
BF16 = mybir.dt.bfloat16
U32 = mybir.dt.uint32
U16 = mybir.dt.uint16
U8 = mybir.dt.uint8
FP8X4 = mybir.dt.float8_e4m3fn_x4
MULT = mybir.AluOpType.mult
SILU = mybir.ActivationFunctionType.Silu

P = 128
CH = 256
NCH = S // CH
NT = 128


def tile_picked_place_mlp_silu_sub_l_kernel(tc, xT, w1, w2, gate, offs, out):
    nc = tc.nc
    with ExitStack() as ctx:
        keep = ctx.enter_context(tc.tile_pool(name="keep", bufs=1))
        hpool = ctx.enter_context(tc.tile_pool(name="hpool", bufs=4))
        ypool = ctx.enter_context(tc.tile_pool(name="ypool", bufs=8))
        psum = ctx.enter_context(tc.psum_pool(name="psum", bufs=4))

        offsets = keep.tile([P, S // 16], U16, name="offsets")
        windows = [keep.tile([P, T], F32, name=f"window{m}") for m in range(2)]
        gates = keep.tile([P, 2, S], F32, name="gates")
        w1_raw = [keep.tile([P, 4, H], F32, name=f"w1_raw{g}") for g in range(2)]
        w2_raw = keep.tile([P, 4, N], F32, name="w2_raw")
        x_raw = [[keep.tile([P, 4, CH], F32, name=f"x_raw{c}_{g}") for g in range(2)] for c in range(NCH)]

        def load_x(c, g):
            src = xT[512 * g : 512 * (g + 1), CH * c : CH * (c + 1)]
            nc.sync.dma_start(out=x_raw[c][g][:], in_=src.rearrange("(p j) s -> p j s", j=4))

        def load_w1(g):
            nc.sync.dma_start(out=w1_raw[g][:], in_=w1[512 * g : 512 * (g + 1), :].rearrange("(p j) h -> p j h", j=4))

        gate_v = gate.rearrange("(m p) s -> p m s", m=2)
        load_w1(0)
        load_w1(1)
        load_x(0, 0)
        load_x(0, 1)
        nc.sync.dma_start(out=w2_raw[:], in_=w2.rearrange("(p j) n -> p j n", j=4))
        load_x(1, 0)
        load_x(1, 1)
        nc.sync.dma_start(offsets[:], offs)
        nc.sync.dma_start(out=gates[:, :, 0:CH], in_=gate_v[:, :, 0:CH])
        load_x(2, 0)
        load_x(2, 1)
        load_x(3, 0)
        load_x(3, 1)
        nc.sync.dma_start(out=gates[:, :, CH:S], in_=gate_v[:, :, CH:S])

        warm = keep.tile([P, 2], F32, name="warm")
        nc.vector.memset(warm[:], 0.0)
        nc.scalar.activation(warm[:, 1:2], warm[:, 0:1], SILU)
        for m in range(2):
            nc.vector.memset(windows[m][:], 0.0)

        w1_grp = [keep.tile([P, 4 * H], BF16, name=f"w1_grp{g}", align_bytes=64) for g in range(2)]
        w1_codes = [keep.tile([P, H], U32, name=f"w1_codes{g}", align_bytes=64) for g in range(2)]
        w1_scales = [keep.tile([P, H], U8, name=f"w1_scales{g}", align_bytes=64) for g in range(2)]
        w2_grp = keep.tile([P, N, 4], BF16, name="w2_grp", align_bytes=64)
        w2_codes = keep.tile([P, N], U32, name="w2_codes", align_bytes=64)
        w2_scales = keep.tile([P, N], U8, name="w2_scales", align_bytes=64)
        x_grp = [keep.tile([P, 2, CH, 4], BF16, name=f"x_grp{c}", align_bytes=64) for c in range(NCH)]
        x_codes = [keep.tile([P, 2, CH], U32, name=f"x_codes{c}", align_bytes=64) for c in range(NCH)]
        x_scales = [keep.tile([P, 2, CH], U8, name=f"x_scales{c}", align_bytes=64) for c in range(NCH)]

        def copy_on(engine, dst, src):
            if engine == "v":
                nc.vector.tensor_copy(out=dst, in_=src)
            else:
                nc.scalar.copy(out=dst, in_=src)

        def quantize(codes, scales, grouped):
            nc.vector.quantize_mx(out=codes.bitcast(FP8X4), scales=scales, in_=grouped)

        def copy_w1(g, engine, m0, m1):
            dst = w1_grp[g][:].rearrange("p (t m j) -> p m j t", t=4, j=4)
            src = w1_raw[g][:].rearrange("p j (m t) -> p m j t", t=4)
            copy_on(engine, dst[:, m0:m1], src[:, m0:m1])

        def copy_x(c, g, engine, a, b):
            dst = x_grp[c][:, g, a:b, :].rearrange("p (n i) j -> p n j i", i=4)
            src = x_raw[c][g][:, :, a:b].rearrange("p j (n i) -> p n j i", i=4)
            copy_on(engine, dst, src)

        def quant_x(c, g, a, b):
            quantize(x_codes[c][:, g, a:b], x_scales[c][:, g, a:b], x_grp[c][:, g, a:b, :].rearrange("p n j -> p (n j)"))

        def quant_x_both(c):
            quantize(
                x_codes[c][:].rearrange("p g n -> p (g n)"),
                x_scales[c][:].rearrange("p g n -> p (g n)"),
                x_grp[c][:].rearrange("p g n j -> p (g n j)"),
            )

        def layer1(c):
            banks = []
            for b in range(CH // NT):
                bank = psum.tile([P, 4, NT], F32, name="h_bank")
                cols = slice(NT * b, NT * (b + 1))
                for t in range(4):
                    for g in range(2):
                        nc.tensor.matmul_mx(
                            out=bank[:, t, :],
                            lhsT=w1_codes[g][:, P * t : P * (t + 1)].bitcast(FP8X4),
                            lhsT_scale=w1_scales[g][:, P * t : P * (t + 1)],
                            rhs=x_codes[c][:, g, cols].bitcast(FP8X4),
                            rhs_scale=x_scales[c][:, g, cols],
                            start=(g == 0),
                            stop=(g == 1),
                        )
                banks.append(bank)
            return banks

        def silu(banks):
            h_grp = hpool.tile([P, CH, 4], BF16, name="h_grp", align_bytes=64)
            for b in range(CH // NT):
                nc.scalar.activation(h_grp[:, NT * b : NT * (b + 1), :], banks[b][:].rearrange("p t n -> p n t"), SILU)
            return h_grp

        def quant_h(h_grp):
            codes = hpool.tile([P, CH], U32, name="h_codes", align_bytes=64)
            scales = hpool.tile([P, CH], U8, name="h_scales", align_bytes=64)
            quantize(codes[:], scales[:], h_grp[:].rearrange("p n j -> p (n j)"))
            return codes, scales

        def layer2(hq, m):
            codes, scales = hq
            y_bank = psum.tile([P, CH], F32, name="y_bank")
            nc.tensor.matmul_mx(
                out=y_bank[:],
                lhsT=w2_codes[:, P * m : P * (m + 1)].bitcast(FP8X4),
                lhsT_scale=w2_scales[:, P * m : P * (m + 1)],
                rhs=codes[:].bitcast(FP8X4),
                rhs_scale=scales[:],
                start=True,
                stop=True,
            )
            return y_bank

        def fetch(y_bank):
            y = ypool.tile([P, CH], F32, name="y")
            nc.scalar.copy(out=y[:], in_=y_bank[:])
            return y

        def copy_w2(engine, a, b):
            dst = w2_grp[:, a:b, :].rearrange("p (n i) j -> p n j i", i=4)
            src = w2_raw[:, :, a:b].rearrange("p j (n i) -> p n j i", i=4)
            copy_on(engine, dst, src)

        def store(m):
            nc.sync.dma_start(out=out[P * m : P * (m + 1), :], in_=windows[m][:])

        def scatter(c, m, y):
            ents = offsets[:, CH // 16 * c : CH // 16 * (c + 1)]
            nc.vector.tensor_tensor(windows[m][:].indirect(ents), y[:], gates[:, m, CH * c : CH * (c + 1)], MULT)

        A, B, AB = (0, 128), (128, 256), (0, 256)
        copy_w1(0, "v", 0, 64)
        copy_w1(0, "s", 64, 128)
        quantize(w1_codes[0][:], w1_scales[0][:], w1_grp[0][:])
        copy_w1(1, "v", 0, 64)
        copy_w1(1, "s", 64, 128)
        copy_x(0, 0, "v", *A)
        copy_x(0, 0, "s", *B)
        quantize(w1_codes[1][:], w1_scales[1][:], w1_grp[1][:])
        quant_x(0, 0, *AB)
        copy_x(0, 1, "v", *A)
        copy_x(0, 1, "s", *B)
        quant_x(0, 1, *A)
        quant_x(0, 1, *B)
        banks0 = layer1(0)
        copy_w2("v", *B)
        copy_w2("s", *A)
        quantize(w2_codes[:], w2_scales[:], w2_grp[:].rearrange("p n j -> p (n j)"))
        h0 = silu(banks0)
        copy_x(1, 0, "v", *AB)
        copy_x(1, 1, "v", *B)
        copy_x(1, 1, "s", *A)
        quant_x(1, 0, *AB)
        hq0 = quant_h(h0)
        y_bank00 = layer2(hq0, 0)
        y_bank01 = layer2(hq0, 1)
        quant_x(1, 1, *AB)
        banks1 = layer1(1)
        y00 = fetch(y_bank00)
        copy_x(2, 0, "s", *B)
        copy_x(2, 0, "v", *A)
        scatter(0, 0, y00)
        h1 = silu(banks1)
        copy_x(2, 1, "s", *B)
        y01 = fetch(y_bank01)
        copy_x(2, 1, "v", *A)
        hq1 = quant_h(h1)
        y_bank10 = layer2(hq1, 0)
        y_bank11 = layer2(hq1, 1)
        quant_x_both(2)
        banks2 = layer1(2)
        copy_x(3, 0, "s", *AB)
        scatter(0, 1, y01)
        copy_x(3, 1, "s", *A)
        copy_x(3, 1, "v", *B)
        y10 = fetch(y_bank10)
        y11 = fetch(y_bank11)
        quant_x_both(3)
        banks3 = layer1(3)
        scatter(1, 0, y10)
        h2 = silu(banks2)
        h3 = silu(banks3)
        hq2 = quant_h(h2)
        y_bank20 = layer2(hq2, 0)
        y_bank21 = layer2(hq2, 1)
        scatter(1, 1, y11)
        y20 = fetch(y_bank20)
        y21 = fetch(y_bank21)
        hq3 = quant_h(h3)
        y_bank30 = layer2(hq3, 0)
        y_bank31 = layer2(hq3, 1)
        scatter(2, 0, y20)
        y30 = fetch(y_bank30)
        y31 = fetch(y_bank31)
        scatter(3, 0, y30)
        store(0)
        scatter(2, 1, y21)
        scatter(3, 1, y31)
        store(1)
